import numpy as np
import ml_dtypes


def mxq(x, axis, fmt="e4m3"):
    dtype, down = {"e4m3": (ml_dtypes.float8_e4m3fn, 7), "e5m2": (ml_dtypes.float8_e5m2, 14)}[fmt]
    v = np.moveaxis(np.asarray(x, np.float32).astype(ml_dtypes.bfloat16).astype(np.float64), axis, -1)
    blocks = v.reshape(v.shape[:-1] + (-1, 32))
    amax = np.abs(blocks).max(-1, keepdims=True)
    byte = np.maximum(np.where(amax > 0, np.frexp(amax)[1] - 1 + 127, 0) - down, 1)
    scale = np.exp2(byte - 127.0)
    codes = (blocks / scale).astype(np.float32).astype(dtype).astype(np.float64)
    return np.moveaxis((codes * scale).reshape(v.shape), -1, axis)


WIDE = False


def mx_kscale(k):
    if not WIDE:
        return np.ones(k)
    levels = np.array([10, -10, 5, -5, 0])
    if k % 512:
        return np.exp2(np.random.permutation(np.resize(levels, k // 32))).repeat(32)
    a = np.empty((k // 512, 16))
    for p in range(k // 512):
        a[p, :8] = np.random.permutation(np.resize(levels, 8))
        for g in range(8):
            far = levels[np.abs(levels - a[p, g]) >= 10]
            a[p, g + 8] = far[np.random.randint(len(far))]
    return np.exp2(a.ravel()).repeat(32)


def f64(x):
    return np.asarray(x).astype(np.float64)


def striped(idx):
    return np.tile(idx.reshape(-1, 16).T, (8, 1)).astype(np.uint16)


def unstriped(offs):
    return offs[:16].T.reshape(-1).astype(np.int64)


def striped8(idx):
    return np.concatenate([x.reshape(-1, 16).T for x in idx]).astype(np.uint16)


def runs(offs, k):
    lists = np.stack([offs[16 * r : 16 * r + 16].T.reshape(-1) for r in range(8)]).astype(np.int64)
    return lists[np.arange(k) % 512 // 64]


def pack_weight(w):
    k, n = w.shape
    w = f64(np.asarray(w, np.float32).astype(ml_dtypes.bfloat16)).reshape(k // 32, 32, n)
    amax = np.abs(w).max(1)
    byte = np.clip(np.where(amax > 0, np.frexp(amax)[1] - 1 + 127 - 7, 1), 1, 254)
    scaled = (w * np.exp2(127.0 - byte)[:, None, :]).reshape(k, n).astype(np.float32)
    words = np.ascontiguousarray(scaled.reshape(k // 512, 128, 4, n).transpose(0, 1, 3, 2)).astype(ml_dtypes.float8_e4m3fn).view(np.uint8)
    return words, np.ascontiguousarray(byte.astype(np.uint8).reshape(k // 512, 16, n))


def unpack_weight(words, scales):
    g, p, n, _ = words.shape
    vals = np.ascontiguousarray(words).view(ml_dtypes.float8_e4m3fn).astype(np.float64) * np.repeat(np.exp2(scales.astype(np.float64) - 127.0), 8, axis=1)[..., None]
    return vals.transpose(0, 1, 3, 2).reshape(g * 512, n)

def planes(y):
    n, m = y.shape
    v = y.astype(np.float32).astype(ml_dtypes.bfloat16).astype(np.float64).reshape(n // 32, 32, m)
    top = np.abs(v).max(1)
    byte = np.clip(np.where(top > 0, np.frexp(top)[1] - 1 + 127 - 7, 1), 1, 254)
    codes = (v * np.exp2(127.0 - byte)[:, None, :]).reshape(n, m).astype(np.float32).astype(ml_dtypes.float8_e4m3fn).view(np.uint8)
    words = codes.reshape(n // 512, 128, 4, m).transpose(0, 1, 3, 2)
    return np.ascontiguousarray(words), np.ascontiguousarray(byte.astype(np.uint8).reshape(n // 512, 16, m))


K, T, S, N, G, H = 512, 1024, 256, 512, 2048, 512


def setup_inputs():
    n = np.random.standard_normal
    s = mx_kscale(K)[:, None]
    u = mx_kscale(K)
    packed_xT = pack_weight(n((K, T)) * s)
    packed_dT = pack_weight(n((K, G)) / s)
    packed_w1 = pack_weight(n((H, N)) / np.sqrt(2 * H) / u[:, None])
    packed_w2 = pack_weight(n((K, N)) / np.sqrt(2 * K) / s)
    return {
        "x_words": packed_xT[0],
        "x_scales": packed_xT[1],
        "d_words": packed_dT[0],
        "d_scales": packed_dT[1],
        "gn": (np.random.uniform(0.5, 1.5, (H, 1)) * u[:, None]).astype(np.float32),
        "w1_words": packed_w1[0],
        "w1_scales": packed_w1[1],
        "w2_words": packed_w2[0],
        "w2_scales": packed_w2[1],
        "offs": striped(np.random.permutation(T)[:S]),
        "k1": striped8(np.random.randint(0, G, (8, H))),
        "n1": striped8(np.stack([np.random.permutation(S) for _ in range(8)])),
        "n2": striped8(np.stack([np.random.permutation(S) for _ in range(8)])),
        "n3": striped8(np.stack([np.random.permutation(S) for _ in range(8)])),
        "two": striped(np.random.permutation(T)[:S]),
        "n4": striped(np.random.permutation(S)),
        "n5": striped(np.random.permutation(S)),
        "n6": striped(np.random.permutation(S)),
    }


def reference(x_words, x_scales, d_words, d_scales, gn, w1_words, w1_scales, w2_words, w2_scales, offs, k1, n1, n2, n3, two, n4, n5, n6):
    d_k1 = unpack_weight(d_words, d_scales)[np.arange(K)[:, None], runs(k1, K)]
    xq = unpack_weight(x_words, x_scales)[:, unstriped(offs)]
    h = 0.0625 * (d_k1.T @ xq)
    st = h - (h[np.arange(H)[:, None], runs(n1, H)])
    su = np.maximum(st, st[np.arange(H)[:, None], runs(n2, H)])
    z = f64(gn) * (su + 0.5 * (su[np.arange(H)[:, None], runs(n3, H)]))
    x_two = unpack_weight(x_words, x_scales)[:, unstriped(two)]
    h2 = unpack_weight(w1_words, w1_scales).T @ mxq(z, 0, "e4m3") + unpack_weight(w2_words, w2_scales).T @ x_two
    out_0 = h2 + h2[:, unstriped(n4)] - (np.maximum(h2[:, unstriped(n5)], h2[:, unstriped(n6)]))
    return (out_0,) + planes(out_0)

@@ -1,0 +1,218 @@
+from contextlib import ExitStack
+
+import concourse.mybir as mybir
+
+K, T, S, N, G, H = 512, 1024, 256, 512, 2048, 512
+FLOPS = 2 * S * (K * H + H * N + K * N)
+
+F32 = mybir.dt.float32
+BF16 = mybir.dt.bfloat16
+I32 = mybir.dt.int32
+U32 = mybir.dt.uint32
+U16 = mybir.dt.uint16
+U8 = mybir.dt.uint8
+FP8X4 = mybir.dt.float8_e4m3fn_x4
+ALU = mybir.AluOpType
+COPY = mybir.ActivationFunctionType.Copy
+
+P = 128
+PACK = 4
+QUADS = 4
+HALF = S // 2
+PIECES = ((0, 128), (128, 192), (192, 256))
+
+
+def as_words(dram_words):
+    return dram_words[0].rearrange("p n r -> p (n r)").bitcast(I32)
+
+
+def tile_picked_pqmixthreetrim_none_po_kernel(
+    tc, x_words, x_scales, d_words, d_scales, gn, w1_words, w1_scales, w2_words, w2_scales,
+    offs, k1, n1, n2, n3, two, n4, n5, n6, out_0, out_1, out_2,
+):
+    nc = tc.nc
+    with ExitStack() as ctx:
+        lists = ctx.enter_context(tc.tile_pool(name="lists", bufs=1))
+        sb = ctx.enter_context(tc.tile_pool(name="sb", bufs=1))
+        psum = ctx.enter_context(tc.psum_pool(name="psum", bufs=1))
+
+        def new(name, shape, dtype, tag=None):
+            return sb.tile(shape, dtype, name=name, tag=tag or name, align_bytes=64)
+
+        def load_list(name, dram):
+            tile = lists.tile([P, dram.shape[1]], U16, name=name)
+            nc.sync.dma_start(tile[:], dram)
+            return tile
+
+        def cols16(lo, hi):
+            return slice(lo // 16, hi // 16)
+
+        d_sc = new("d_sc", [P, G], U8, tag="d_sc_then_w1")
+        nc.vector.memset(d_sc[:].bitcast(I32), 0)
+        x_sc = new("x_sc", [P, T], U8)
+        nc.gpsimd.memset(x_sc[:].bitcast(I32), 0)
+        d_plane = new("d_plane", [P, H], U8, tag="d_plane_then_x2")
+        nc.vector.memset(d_plane[:].bitcast(I32), 0)
+        ping = [new("ping%d" % t, [P, 2 * S], F32) for t in range(PACK)]
+        pong = [new("pong%d" % t, [P, 2 * S], F32) for t in range(PACK)]
+        for t in range(PACK):
+            nc.vector.memset(ping[t][:, S:], 0.0)
+
+        k1_t = load_list("k1_t", k1)
+        nc.scalar.dma_start(d_sc[0:P:8, :].bitcast(I32), d_scales[0].bitcast(I32))
+        d_w = new("d_w", [P, G], I32)
+        nc.sync.dma_start(d_w[:], as_words(d_words))
+        offs_t = load_list("offs_t", offs)
+        x_w = new("x_w", [P, T], I32)
+        nc.sync.dma_start(x_w[:], as_words(x_words))
+        for q in range(QUADS):
+            nc.scalar.dma_start(x_sc[32 * q : 32 * q + 4, :].bitcast(I32), x_scales[0, 4 * q : 4 * q + 4, :].bitcast(I32))
+        two_t = load_list("two_t", two)
+        n1_t = load_list("n1_t", n1)
+        n2_t = load_list("n2_t", n2)
+        n3_t = load_list("n3_t", n3)
+        n5_t = load_list("n5_t", n5)
+        n6_t = load_list("n6_t", n6)
+        n4_t = load_list("n4_t", n4)
+        gain = new("gain", [P, PACK], F32)
+        nc.gpsimd.dma_start(gain[:], gn.rearrange("(p t) o -> p (t o)", t=PACK))
+
+        d_sc_picked = new("d_sc_picked", [P, H], U8, tag="d_sc_picked_then_w2")
+        nc.vector.tensor_copy(d_sc_picked[:], d_sc[:].indirect(k1_t[:]))
+        d_sc_dealt = new("d_sc_dealt", [P, H], U8, tag="d_sc_dealt_then_w_sc")
+        nc.vector.tensor_copy(
+            d_sc_dealt[:].rearrange("p (t m) -> p t m", t=PACK), d_sc_picked[:].rearrange("p (m t) -> p t m", t=PACK)
+        )
+        for q in range(QUADS):
+            nc.scalar.dma_start(
+                d_plane[32 * q : 32 * q + 4, :].bitcast(I32), d_sc_dealt[32 * q : 32 * q + 32 : 8, :].bitcast(I32)
+            )
+        w_raw = [new("w1_raw", [P, N], I32, tag="d_sc_then_w1"), new("w2_raw", [P, N], I32, tag="d_sc_picked_then_w2")]
+        nc.sync.dma_start(w_raw[0][:], as_words(w1_words))
+        nc.sync.dma_start(w_raw[1][:], as_words(w2_words))
+        w_sc = new("w_sc", [P, N], U8, tag="d_sc_dealt_then_w_sc")
+        nc.gpsimd.memset(w_sc[:].bitcast(I32), 0)
+        for a, scales in enumerate((w1_scales, w2_scales)):
+            for q in range(QUADS):
+                row = 32 * q + 4 * a
+                nc.sync.dma_start(w_sc[row : row + 4, :].bitcast(I32), scales[0, 4 * q : 4 * q + 4, :].bitcast(I32))
+
+        d_w_picked = new("d_w_picked", [P, H], U32)
+        nc.vector.tensor_copy(d_w_picked[:], d_w[:].bitcast(U32).indirect(k1_t[:]))
+        d_w_dealt = new("d_w_dealt", [P, H], I32, tag="d_w_dealt_then_w1")
+        nc.vector.tensor_copy(
+            d_w_dealt[:].rearrange("p (t m) -> p t m", t=PACK),
+            d_w_picked[:].bitcast(I32).rearrange("p (m t) -> p t m", t=PACK),
+        )
+        x1_sc = new("x1_sc", [P, S], U8)
+        nc.vector.tensor_copy(x1_sc[:], x_sc[:].indirect(offs_t[:]))
+        x1_w = new("x1_w", [P, S], U32, tag="x1_w_then_w2")
+        nc.vector.tensor_copy(x1_w[:], x_w[:].bitcast(U32).indirect(offs_t[:]))
+        x2_sc = new("x2_sc", [P, S], U8)
+        nc.vector.tensor_copy(x2_sc[:], x_sc[:].indirect(two_t[:]))
+
+        for t in range(PACK):
+            cols = slice(P * t, P * (t + 1))
+            h_ps = psum.tile([P, S], F32, name="h_ps%d" % t, tag="bank%d" % t)
+            nc.tensor.matmul_mx(
+                h_ps[:], lhsT=d_w_dealt[:, cols].bitcast(FP8X4), lhsT_scale=d_plane[:, cols],
+                rhs=x1_w[:].bitcast(FP8X4), rhs_scale=x1_sc[:], start=True, stop=True,
+            )
+            nc.vector.tensor_scalar(ping[t][:, :S], h_ps[:], 0.0625, None, ALU.mult)
+
+        for t in range(PACK):
+            nc.scalar.activation(pong[t][:, S:], ping[t][:].indirect(n1_t[:]), COPY)
+            nc.vector.tensor_tensor(pong[t][:, :S], ping[t][:, :S], pong[t][:, S:], ALU.subtract)
+
+        half_gain = new("half_gain", [P, PACK], F32)
+        nc.vector.tensor_scalar(half_gain[:], gain[:], 0.5, None, ALU.mult)
+        su_gain = new("su_gain", [P, PACK, S], F32)
+        su_half = [new("su_half%d" % t, [P, S], F32) for t in range(PACK)]
+        for t in range(PACK):
+            nc.scalar.activation(ping[t][:, S:], pong[t][:].indirect(n2_t[:]), COPY)
+            nc.vector.tensor_tensor(ping[t][:, :S], pong[t][:, :S], ping[t][:, S:], ALU.max)
+            nc.vector.tensor_scalar(su_half[t][:], ping[t][:, :S], half_gain[:, t : t + 1], None, ALU.mult)
+            nc.vector.tensor_scalar(su_gain[:, t, :], ping[t][:, :S], gain[:, t : t + 1], None, ALU.mult)
+
+        x2_w = new("x2_w", [P, S], U32, tag="d_plane_then_x2")
+        nc.vector.tensor_copy(x2_w[:], x_w[:].bitcast(U32).indirect(two_t[:]))
+        w_dealt = [new("w1_dealt", [P, N], I32, tag="d_w_dealt_then_w1"), new("w2_dealt", [P, N], I32, tag="x1_w_then_w2")]
+        for a in (1, 0):
+            nc.vector.tensor_copy(
+                w_dealt[a][:].rearrange("p (t m) -> p t m", t=PACK), w_raw[a][:].rearrange("p (m t) -> p t m", t=PACK)
+            )
+        w_plane = new("w_plane", [P, N], U8)
+        nc.vector.tensor_copy(
+            w_plane[:].rearrange("p (t m) -> p t m", t=PACK), w_sc[:].rearrange("p (m t) -> p t m", t=PACK)
+        )
+        h2_ps = [
+            [psum.tile([P, HALF], F32, name="h2_ps%d_%d" % (u, t), tag="bank%d" % (PACK * (1 - u) + t)) for t in range(PACK)]
+            for u in range(2)
+        ]
+        for u in range(2):
+            places = slice(HALF * u, HALF * (u + 1))
+            for t in range(PACK):
+                cols = slice(P * t, P * (t + 1))
+                nc.tensor.matmul_mx(
+                    h2_ps[u][t][:], lhsT=w_dealt[1][:, cols].bitcast(FP8X4), lhsT_scale=w_plane[4:, cols],
+                    rhs=x2_w[:, places].bitcast(FP8X4), rhs_scale=x2_sc[:, places], start=True, stop=False,
+                )
+
+        z_w = new("z_w", [P, S], U32)
+        z_sc = new("z_sc", [P, S], U8)
+        for lo, hi in PIECES:
+            picked = new("su_picked%d" % lo, [P, PACK, hi - lo], F32)
+            for t in range(PACK):
+                nc.scalar.activation(picked[:, t, :], su_half[t][:].indirect(n3_t[:, cols16(lo, hi)]), COPY)
+            z_bf = new("z_bf%d" % lo, [P, PACK * (hi - lo)], BF16)
+            nc.vector.tensor_tensor(
+                z_bf[:].rearrange("p (c i t) -> p c t i", i=4, t=PACK),
+                su_gain[:, :, lo:hi].rearrange("p t (c i) -> p c t i", i=4),
+                picked[:].rearrange("p t (c i) -> p c t i", i=4),
+                ALU.add,
+            )
+            nc.vector.quantize_mx(z_w[:, lo:hi].bitcast(FP8X4), z_sc[:, lo:hi], z_bf[:])
+            if hi % HALF == 0:
+                u = hi // HALF - 1
+                places = slice(HALF * u, HALF * (u + 1))
+                for t in range(PACK):
+                    cols = slice(P * t, P * (t + 1))
+                    nc.tensor.matmul_mx(
+                        h2_ps[u][t][:], lhsT=w_dealt[0][:, cols].bitcast(FP8X4), lhsT_scale=w_plane[:, cols],
+                        rhs=z_w[:, places].bitcast(FP8X4), rhs_scale=z_sc[:, places], start=False, stop=True,
+                    )
+
+        for t in range(PACK):
+            nc.scalar.activation(ping[t][:, :HALF], h2_ps[0][t][:], COPY)
+        for t in range(PACK):
+            nc.vector.tensor_copy(ping[t][:, HALF:S], h2_ps[1][t][:])
+
+        trimmed = new("trimmed", [P, PACK, S], F32)
+        for t in range(PACK):
+            nc.scalar.activation(pong[t][:, :S], ping[t][:].indirect(n5_t[:]), COPY)
+            nc.scalar.activation(pong[t][:, S:], ping[t][:].indirect(n6_t[:]), COPY)
+            larger = new("larger%d" % t, [P, S], F32)
+            nc.vector.tensor_tensor(larger[:], pong[t][:, :S], pong[t][:, S:], ALU.max)
+            nc.vector.tensor_tensor(trimmed[:, t, :], ping[t][:, :S], larger[:], ALU.subtract)
+
+        y_w = new("y_w", [P, S], U32)
+        y_sc = new("y_sc", [P, S], U8)
+        out_rows = out_0.rearrange("(p t) j -> p t j", t=PACK)
+        out_words = as_words(out_1)
+        for lo, hi in PIECES:
+            picked = new("h2_picked%d" % lo, [P, PACK, hi - lo], F32)
+            for t in range(PACK):
+                nc.scalar.activation(picked[:, t, :], ping[t][:].indirect(n4_t[:, cols16(lo, hi)]), COPY)
+            y = new("y%d" % lo, [P, PACK, hi - lo], F32)
+            nc.vector.tensor_tensor(y[:], trimmed[:, :, lo:hi], picked[:], ALU.add)
+            nc.sync.dma_start(out_rows[:, :, lo:hi], y[:])
+            y_bf = new("y_bf%d" % lo, [P, PACK * (hi - lo)], BF16)
+            nc.vector.tensor_copy(
+                y_bf[:].rearrange("p (c i t) -> p c t i", i=4, t=PACK), y[:].rearrange("p t (c i) -> p c t i", i=4)
+            )
+            nc.vector.quantize_mx(y_w[:, lo:hi].bitcast(FP8X4), y_sc[:, lo:hi], y_bf[:])
+            if hi % HALF == 0:
+                places = slice(hi - HALF, hi)
+                nc.sync.dma_start(out_words[:, places], y_w[:, places].bitcast(I32))
+        for q in range(QUADS):
+            nc.scalar.dma_start(out_2[0, 4 * q : 4 * q + 4, :].bitcast(I32), y_sc[32 * q : 32 * q + 4, :].bitcast(I32))

@@ -20,6 +20,7 @@ PACK = 4
 QUADS = 4
 HALF = S // 2
 PIECES = ((0, 128), (128, 192), (192, 256))
+LAST = 64
 
 
 def as_words(dram_words):
@@ -47,26 +48,40 @@ def tile_picked_pqmixthreetrim_none_po_kernel(
         def cols16(lo, hi):
             return slice(lo // 16, hi // 16)
 
-        d_sc = new("d_sc", [P, G], U8, tag="d_sc_then_w1")
-        nc.vector.memset(d_sc[:].bitcast(I32), 0)
-        x_sc = new("x_sc", [P, T], U8)
-        nc.gpsimd.memset(x_sc[:].bitcast(I32), 0)
-        d_plane = new("d_plane", [P, H], U8, tag="d_plane_then_x2")
-        nc.vector.memset(d_plane[:].bitcast(I32), 0)
+        def spread_rows(dram_scales):
+            words = dram_scales[0].bitcast(I32)
+            return words.unsqueeze(1).to_broadcast([16, 8, words.shape[1]])
+
+        def deal(out, in_, run):
+            nc.vector.tensor_copy(
+                out.rearrange("p (t c i) -> p c t i", t=PACK, i=run), in_.rearrange("p (c i t) -> p c t i", t=PACK, i=run)
+            )
+
+        def place_rows(plane, staged):
+            for q in range(QUADS):
+                nc.scalar.dma_start(
+                    plane[32 * q : 32 * q + 4, :].bitcast(I32), staged[32 * q : 32 * q + 32 : 8, :].bitcast(I32)
+                )
+
+        plane1 = new("plane1", [P, H + S], U8, tag="plane1_then_staged2")
+        nc.vector.memset(plane1[:].bitcast(I32), 0)
+        plane2 = new("plane2", [P, 2 * N + S], U8)
+        nc.vector.memset(plane2[:].bitcast(I32), 0)
         ping = [new("ping%d" % t, [P, 2 * S], F32) for t in range(PACK)]
         pong = [new("pong%d" % t, [P, 2 * S], F32) for t in range(PACK)]
         for t in range(PACK):
             nc.vector.memset(ping[t][:, S:], 0.0)
 
         k1_t = load_list("k1_t", k1)
-        nc.scalar.dma_start(d_sc[0:P:8, :].bitcast(I32), d_scales[0].bitcast(I32))
-        d_w = new("d_w", [P, G], I32)
-        nc.sync.dma_start(d_w[:], as_words(d_words))
+        d_sc = new("d_sc", [P, G], U8)
+        nc.sync.dma_start(d_sc[:].bitcast(I32), spread_rows(d_scales))
         offs_t = load_list("offs_t", offs)
+        x_sc = new("x_sc", [P, T], U8)
+        nc.sync.dma_start(x_sc[:].bitcast(I32), spread_rows(x_scales))
+        d_w = new("d_w", [P, G], I32, tag="d_w_then_w1")
+        nc.sync.dma_start(d_w[:], as_words(d_words))
         x_w = new("x_w", [P, T], I32)
         nc.sync.dma_start(x_w[:], as_words(x_words))
-        for q in range(QUADS):
-            nc.scalar.dma_start(x_sc[32 * q : 32 * q + 4, :].bitcast(I32), x_scales[0, 4 * q : 4 * q + 4, :].bitcast(I32))
         two_t = load_list("two_t", two)
         n1_t = load_list("n1_t", n1)
         n2_t = load_list("n2_t", n2)
@@ -74,77 +89,72 @@ def tile_picked_pqmixthreetrim_none_po_kernel(
         n5_t = load_list("n5_t", n5)
         n6_t = load_list("n6_t", n6)
         n4_t = load_list("n4_t", n4)
+        w_sc = new("w_sc", [P, 2 * N], U8)
+        nc.gpsimd.memset(w_sc[:].bitcast(I32), 0)
+        nc.gpsimd.dma_start(w_sc[0:P:8, :N].bitcast(I32), w1_scales[0].bitcast(I32))
+        nc.gpsimd.dma_start(w_sc[0:P:8, N:].bitcast(I32), w2_scales[0].bitcast(I32))
         gain = new("gain", [P, PACK], F32)
         nc.gpsimd.dma_start(gain[:], gn.rearrange("(p t) o -> p (t o)", t=PACK))
 
-        d_sc_picked = new("d_sc_picked", [P, H], U8, tag="d_sc_picked_then_w2")
+        d_sc_picked = new("d_sc_picked", [P, H], U8)
         nc.vector.tensor_copy(d_sc_picked[:], d_sc[:].indirect(k1_t[:]))
-        d_sc_dealt = new("d_sc_dealt", [P, H], U8, tag="d_sc_dealt_then_w_sc")
-        nc.vector.tensor_copy(
-            d_sc_dealt[:].rearrange("p (t m) -> p t m", t=PACK), d_sc_picked[:].rearrange("p (m t) -> p t m", t=PACK)
-        )
-        for q in range(QUADS):
-            nc.scalar.dma_start(
-                d_plane[32 * q : 32 * q + 4, :].bitcast(I32), d_sc_dealt[32 * q : 32 * q + 32 : 8, :].bitcast(I32)
-            )
-        w_raw = [new("w1_raw", [P, N], I32, tag="d_sc_then_w1"), new("w2_raw", [P, N], I32, tag="d_sc_picked_then_w2")]
-        nc.sync.dma_start(w_raw[0][:], as_words(w1_words))
-        nc.sync.dma_start(w_raw[1][:], as_words(w2_words))
-        w_sc = new("w_sc", [P, N], U8, tag="d_sc_dealt_then_w_sc")
-        nc.gpsimd.memset(w_sc[:].bitcast(I32), 0)
-        for a, scales in enumerate((w1_scales, w2_scales)):
-            for q in range(QUADS):
-                row = 32 * q + 4 * a
-                nc.sync.dma_start(w_sc[row : row + 4, :].bitcast(I32), scales[0, 4 * q : 4 * q + 4, :].bitcast(I32))
-
-        d_w_picked = new("d_w_picked", [P, H], U32)
-        nc.vector.tensor_copy(d_w_picked[:], d_w[:].bitcast(U32).indirect(k1_t[:]))
-        d_w_dealt = new("d_w_dealt", [P, H], I32, tag="d_w_dealt_then_w1")
-        nc.vector.tensor_copy(
-            d_w_dealt[:].rearrange("p (t m) -> p t m", t=PACK),
-            d_w_picked[:].bitcast(I32).rearrange("p (m t) -> p t m", t=PACK),
-        )
         x1_sc = new("x1_sc", [P, S], U8)
         nc.vector.tensor_copy(x1_sc[:], x_sc[:].indirect(offs_t[:]))
+        staged1 = new("staged1", [P, H + S], U8)
+        deal(staged1[:, :H], d_sc_picked[:], 16)
+        nc.vector.tensor_copy(staged1[:, H:].bitcast(I32), x1_sc[:].bitcast(I32))
+        place_rows(plane1, staged1)
+
+        d_w_picked = new("d_w_picked", [P, H], U32, tag="d_w_picked_then_w2")
+        nc.vector.tensor_copy(d_w_picked[:], d_w[:].bitcast(U32).indirect(k1_t[:]))
         x1_w = new("x1_w", [P, S], U32, tag="x1_w_then_w2")
         nc.vector.tensor_copy(x1_w[:], x_w[:].bitcast(U32).indirect(offs_t[:]))
-        x2_sc = new("x2_sc", [P, S], U8)
-        nc.vector.tensor_copy(x2_sc[:], x_sc[:].indirect(two_t[:]))
+        d_w_dealt = new("d_w_dealt", [P, H], I32, tag="d_w_dealt_then_w1")
+        deal(d_w_dealt[:], d_w_picked[:].bitcast(I32), 4)
+
+        w_raw = [new("w1_raw", [P, N], I32, tag="d_w_then_w1"), new("w2_raw", [P, N], I32, tag="d_w_picked_then_w2")]
+        nc.sync.dma_start(w_raw[0][:], as_words(w1_words))
+        nc.sync.dma_start(w_raw[1][:], as_words(w2_words))
 
         for t in range(PACK):
             cols = slice(P * t, P * (t + 1))
             h_ps = psum.tile([P, S], F32, name="h_ps%d" % t, tag="bank%d" % t)
             nc.tensor.matmul_mx(
-                h_ps[:], lhsT=d_w_dealt[:, cols].bitcast(FP8X4), lhsT_scale=d_plane[:, cols],
-                rhs=x1_w[:].bitcast(FP8X4), rhs_scale=x1_sc[:], start=True, stop=True,
+                h_ps[:], lhsT=d_w_dealt[:, cols].bitcast(FP8X4), lhsT_scale=plane1[:, cols],
+                rhs=x1_w[:].bitcast(FP8X4), rhs_scale=plane1[:, H:], start=True, stop=True,
             )
-            nc.vector.tensor_scalar(ping[t][:, :S], h_ps[:], 0.0625, None, ALU.mult)
+            if t < 2:
+                nc.scalar.activation(ping[t][:, :S], h_ps[:], COPY, scale=0.0625)
+            else:
+                nc.vector.tensor_scalar(ping[t][:, :S], h_ps[:], 0.0625, None, ALU.mult)
+        x2_w = new("x2_w", [P, S], U32)
+        nc.vector.tensor_copy(x2_w[:], x_w[:].bitcast(U32).indirect(two_t[:]))
+
+        x2_sc = new("x2_sc", [P, S], U8)
+        nc.vector.tensor_copy(x2_sc[:], x_sc[:].indirect(two_t[:]))
+        staged2 = new("staged2", [P, 2 * N + S], U8, tag="plane1_then_staged2")
+        deal(staged2[:, :N], w_sc[:, :N], 16)
+        deal(staged2[:, N : 2 * N], w_sc[:, N:], 16)
+        nc.vector.tensor_copy(staged2[:, 2 * N :].bitcast(I32), x2_sc[:].bitcast(I32))
+        for q in range(QUADS):
+            nc.sync.dma_start(
+                plane2[32 * q : 32 * q + 4, :].bitcast(I32), staged2[32 * q : 32 * q + 32 : 8, :].bitcast(I32)
+            )
 
         for t in range(PACK):
             nc.scalar.activation(pong[t][:, S:], ping[t][:].indirect(n1_t[:]), COPY)
             nc.vector.tensor_tensor(pong[t][:, :S], ping[t][:, :S], pong[t][:, S:], ALU.subtract)
 
-        half_gain = new("half_gain", [P, PACK], F32)
-        nc.vector.tensor_scalar(half_gain[:], gain[:], 0.5, None, ALU.mult)
+        w_dealt = [new("w1_dealt", [P, N], I32, tag="d_w_dealt_then_w1"), new("w2_dealt", [P, N], I32, tag="x1_w_then_w2")]
         su_gain = new("su_gain", [P, PACK, S], F32)
-        su_half = [new("su_half%d" % t, [P, S], F32) for t in range(PACK)]
+        su = [new("su%d" % t, [P, S], F32) for t in range(PACK)]
         for t in range(PACK):
             nc.scalar.activation(ping[t][:, S:], pong[t][:].indirect(n2_t[:]), COPY)
-            nc.vector.tensor_tensor(ping[t][:, :S], pong[t][:, :S], ping[t][:, S:], ALU.max)
-            nc.vector.tensor_scalar(su_half[t][:], ping[t][:, :S], half_gain[:, t : t + 1], None, ALU.mult)
-            nc.vector.tensor_scalar(su_gain[:, t, :], ping[t][:, :S], gain[:, t : t + 1], None, ALU.mult)
+            nc.vector.tensor_tensor(su[t][:], pong[t][:, :S], ping[t][:, S:], ALU.max)
+            nc.vector.tensor_scalar(su_gain[:, t, :], su[t][:], gain[:, t : t + 1], None, ALU.mult)
+            if t < 2:
+                deal(w_dealt[t][:], w_raw[t][:], 4)
 
-        x2_w = new("x2_w", [P, S], U32, tag="d_plane_then_x2")
-        nc.vector.tensor_copy(x2_w[:], x_w[:].bitcast(U32).indirect(two_t[:]))
-        w_dealt = [new("w1_dealt", [P, N], I32, tag="d_w_dealt_then_w1"), new("w2_dealt", [P, N], I32, tag="x1_w_then_w2")]
-        for a in (1, 0):
-            nc.vector.tensor_copy(
-                w_dealt[a][:].rearrange("p (t m) -> p t m", t=PACK), w_raw[a][:].rearrange("p (m t) -> p t m", t=PACK)
-            )
-        w_plane = new("w_plane", [P, N], U8)
-        nc.vector.tensor_copy(
-            w_plane[:].rearrange("p (t m) -> p t m", t=PACK), w_sc[:].rearrange("p (m t) -> p t m", t=PACK)
-        )
         h2_ps = [
             [psum.tile([P, HALF], F32, name="h2_ps%d_%d" % (u, t), tag="bank%d" % (PACK * (1 - u) + t)) for t in range(PACK)]
             for u in range(2)
@@ -154,8 +164,10 @@ def tile_picked_pqmixthreetrim_none_po_kernel(
             for t in range(PACK):
                 cols = slice(P * t, P * (t + 1))
                 nc.tensor.matmul_mx(
-                    h2_ps[u][t][:], lhsT=w_dealt[1][:, cols].bitcast(FP8X4), lhsT_scale=w_plane[4:, cols],
-                    rhs=x2_w[:, places].bitcast(FP8X4), rhs_scale=x2_sc[:, places], start=True, stop=False,
+                    h2_ps[u][t][:], lhsT=w_dealt[1][:, cols].bitcast(FP8X4),
+                    lhsT_scale=plane2[:, N + P * t : N + P * (t + 1)],
+                    rhs=x2_w[:, places].bitcast(FP8X4),
+                    rhs_scale=plane2[:, 2 * N + HALF * u : 2 * N + HALF * (u + 1)], start=True, stop=False,
                 )
 
         z_w = new("z_w", [P, S], U32)
@@ -163,7 +175,11 @@ def tile_picked_pqmixthreetrim_none_po_kernel(
         for lo, hi in PIECES:
             picked = new("su_picked%d" % lo, [P, PACK, hi - lo], F32)
             for t in range(PACK):
-                nc.scalar.activation(picked[:, t, :], su_half[t][:].indirect(n3_t[:, cols16(lo, hi)]), COPY)
+                for a in range(lo, hi, 64):
+                    nc.scalar.activation(
+                        picked[:, t, a - lo : a - lo + 64], su_gain[:, t, :].indirect(n3_t[:, cols16(a, a + 64)]),
+                        COPY, scale=0.5,
+                    )
             z_bf = new("z_bf%d" % lo, [P, PACK * (hi - lo)], BF16)
             nc.vector.tensor_tensor(
                 z_bf[:].rearrange("p (c i t) -> p c t i", i=4, t=PACK),
@@ -178,7 +194,7 @@ def tile_picked_pqmixthreetrim_none_po_kernel(
                 for t in range(PACK):
                     cols = slice(P * t, P * (t + 1))
                     nc.tensor.matmul_mx(
-                        h2_ps[u][t][:], lhsT=w_dealt[0][:, cols].bitcast(FP8X4), lhsT_scale=w_plane[:, cols],
+                        h2_ps[u][t][:], lhsT=w_dealt[0][:, cols].bitcast(FP8X4), lhsT_scale=plane2[:, cols],
                         rhs=z_w[:, places].bitcast(FP8X4), rhs_scale=z_sc[:, places], start=False, stop=True,
                     )
 
@@ -199,20 +215,37 @@ def tile_picked_pqmixthreetrim_none_po_kernel(
         y_sc = new("y_sc", [P, S], U8)
         out_rows = out_0.rearrange("(p t) j -> p t j", t=PACK)
         out_words = as_words(out_1)
-        for lo, hi in PIECES:
-            picked = new("h2_picked%d" % lo, [P, PACK, hi - lo], F32)
-            for t in range(PACK):
-                nc.scalar.activation(picked[:, t, :], ping[t][:].indirect(n4_t[:, cols16(lo, hi)]), COPY)
-            y = new("y%d" % lo, [P, PACK, hi - lo], F32)
-            nc.vector.tensor_tensor(y[:], trimmed[:, :, lo:hi], picked[:], ALU.add)
-            nc.sync.dma_start(out_rows[:, :, lo:hi], y[:])
+        early = S - LAST
+        picked = new("h2_picked", [P, PACK, early], F32)
+        y = new("y", [P, PACK, early], F32)
+        for t in range(PACK):
+            nc.scalar.activation(picked[:, t, :], ping[t][:].indirect(n4_t[:, cols16(0, early)]), COPY)
+            nc.vector.tensor_tensor(y[:, t, :], trimmed[:, t, :early], picked[:, t, :], ALU.add)
+        nc.sync.dma_start(out_rows[:, :, :early], y[:])
+        for lo, hi in ((0, HALF), (HALF, early)):
             y_bf = new("y_bf%d" % lo, [P, PACK * (hi - lo)], BF16)
             nc.vector.tensor_copy(
-                y_bf[:].rearrange("p (c i t) -> p c t i", i=4, t=PACK), y[:].rearrange("p t (c i) -> p c t i", i=4)
+                y_bf[:].rearrange("p (c i t) -> p c t i", i=4, t=PACK),
+                y[:, :, lo:hi].rearrange("p t (c i) -> p c t i", i=4),
             )
             nc.vector.quantize_mx(y_w[:, lo:hi].bitcast(FP8X4), y_sc[:, lo:hi], y_bf[:])
-            if hi % HALF == 0:
-                places = slice(hi - HALF, hi)
-                nc.sync.dma_start(out_words[:, places], y_w[:, places].bitcast(I32))
+        nc.sync.dma_start(out_words[:, :early], y_w[:, :early].bitcast(I32))
+
+        picked_last = new("h2_picked_last", [P, PACK, LAST], F32)
+        for t in range(PACK):
+            nc.scalar.activation(picked_last[:, t, :], ping[t][:].indirect(n4_t[:, cols16(early, S)]), COPY)
+        y_bf_last = new("y_bf_last", [P, PACK * LAST], BF16)
+        nc.vector.tensor_tensor(
+            y_bf_last[:].rearrange("p (c i t) -> p c t i", i=4, t=PACK),
+            trimmed[:, :, early:].rearrange("p t (c i) -> p c t i", i=4),
+            picked_last[:].rearrange("p t (c i) -> p c t i", i=4),
+            ALU.add,
+        )
+        y_last = new("y_last", [P, PACK, LAST], F32)
+        nc.vector.tensor_tensor(y_last[:], trimmed[:, :, early:], picked_last[:], ALU.add)
+        nc.vector.quantize_mx(y_w[:, early:].bitcast(FP8X4), y_sc[:, early:], y_bf_last[:])
+        nc.scalar.dma_start(out_rows[:, :, early:], y_last[:])
+        nc.sync.dma_start(out_words[:, early:], y_w[:, early:].bitcast(I32))
         for q in range(QUADS):
-            nc.scalar.dma_start(out_2[0, 4 * q : 4 * q + 4, :].bitcast(I32), y_sc[32 * q : 32 * q + 4, :].bitcast(I32))
+            queue = nc.scalar if q % 2 == 0 else nc.sync
+            queue.dma_start(out_2[0, 4 * q : 4 * q + 4, :].bitcast(I32), y_sc[32 * q : 32 * q + 4, :].bitcast(I32))

from contextlib import ExitStack

import concourse.mybir as mybir

K, T, S, N, G, H = 512, 1024, 256, 512, 2048, 512
FLOPS = 2 * S * (K * H + H * N + K * N)

F32 = mybir.dt.float32
BF16 = mybir.dt.bfloat16
I32 = mybir.dt.int32
U32 = mybir.dt.uint32
U16 = mybir.dt.uint16
U8 = mybir.dt.uint8
FP8X4 = mybir.dt.float8_e4m3fn_x4
ALU = mybir.AluOpType
COPY = mybir.ActivationFunctionType.Copy

P = 128
PACK = 4
QUADS = 4
HALF = S // 2
PIECES = ((0, 128), (128, 192), (192, 256))
LAST = 64


def as_words(dram_words):
    return dram_words[0].rearrange("p n r -> p (n r)").bitcast(I32)


def tile_picked_pqmixthreetrim_none_po_kernel(
    tc, x_words, x_scales, d_words, d_scales, gn, w1_words, w1_scales, w2_words, w2_scales,
    offs, k1, n1, n2, n3, two, n4, n5, n6, out_0, out_1, out_2,
):
    nc = tc.nc
    with ExitStack() as ctx:
        lists = ctx.enter_context(tc.tile_pool(name="lists", bufs=1))
        sb = ctx.enter_context(tc.tile_pool(name="sb", bufs=1))
        psum = ctx.enter_context(tc.psum_pool(name="psum", bufs=1))

        def new(name, shape, dtype, tag=None):
            return sb.tile(shape, dtype, name=name, tag=tag or name, align_bytes=64)

        def load_list(name, dram):
            tile = lists.tile([P, dram.shape[1]], U16, name=name)
            nc.sync.dma_start(tile[:], dram)
            return tile

        def cols16(lo, hi):
            return slice(lo // 16, hi // 16)

        def spread_rows(dram_scales):
            words = dram_scales[0].bitcast(I32)
            return words.unsqueeze(1).to_broadcast([16, 8, words.shape[1]])

        def deal(out, in_, run):
            nc.vector.tensor_copy(
                out.rearrange("p (t c i) -> p c t i", t=PACK, i=run), in_.rearrange("p (c i t) -> p c t i", t=PACK, i=run)
            )

        def place_rows(plane, staged):
            for q in range(QUADS):
                nc.scalar.dma_start(
                    plane[32 * q : 32 * q + 4, :].bitcast(I32), staged[32 * q : 32 * q + 32 : 8, :].bitcast(I32)
                )

        plane1 = new("plane1", [P, H + S], U8, tag="plane1_then_staged2")
        nc.vector.memset(plane1[:].bitcast(I32), 0)
        plane2 = new("plane2", [P, 2 * N + S], U8)
        nc.vector.memset(plane2[:].bitcast(I32), 0)
        ping = [new("ping%d" % t, [P, 2 * S], F32) for t in range(PACK)]
        pong = [new("pong%d" % t, [P, 2 * S], F32) for t in range(PACK)]
        for t in range(PACK):
            nc.vector.memset(ping[t][:, S:], 0.0)

        k1_t = load_list("k1_t", k1)
        d_sc = new("d_sc", [P, G], U8)
        nc.sync.dma_start(d_sc[:].bitcast(I32), spread_rows(d_scales))
        offs_t = load_list("offs_t", offs)
        x_sc = new("x_sc", [P, T], U8)
        nc.sync.dma_start(x_sc[:].bitcast(I32), spread_rows(x_scales))
        d_w = new("d_w", [P, G], I32, tag="d_w_then_w1")
        nc.sync.dma_start(d_w[:], as_words(d_words))
        x_w = new("x_w", [P, T], I32)
        nc.sync.dma_start(x_w[:], as_words(x_words))
        two_t = load_list("two_t", two)
        n1_t = load_list("n1_t", n1)
        n2_t = load_list("n2_t", n2)
        n3_t = load_list("n3_t", n3)
        n5_t = load_list("n5_t", n5)
        n6_t = load_list("n6_t", n6)
        n4_t = load_list("n4_t", n4)
        w_sc = new("w_sc", [P, 2 * N], U8)
        nc.gpsimd.memset(w_sc[:].bitcast(I32), 0)
        nc.gpsimd.dma_start(w_sc[0:P:8, :N].bitcast(I32), w1_scales[0].bitcast(I32))
        nc.gpsimd.dma_start(w_sc[0:P:8, N:].bitcast(I32), w2_scales[0].bitcast(I32))
        gain = new("gain", [P, PACK], F32)
        nc.gpsimd.dma_start(gain[:], gn.rearrange("(p t) o -> p (t o)", t=PACK))

        d_sc_picked = new("d_sc_picked", [P, H], U8)
        nc.vector.tensor_copy(d_sc_picked[:], d_sc[:].indirect(k1_t[:]))
        x1_sc = new("x1_sc", [P, S], U8)
        nc.vector.tensor_copy(x1_sc[:], x_sc[:].indirect(offs_t[:]))
        staged1 = new("staged1", [P, H + S], U8)
        deal(staged1[:, :H], d_sc_picked[:], 16)
        nc.vector.tensor_copy(staged1[:, H:].bitcast(I32), x1_sc[:].bitcast(I32))
        place_rows(plane1, staged1)

        d_w_picked = new("d_w_picked", [P, H], U32, tag="d_w_picked_then_w2")
        nc.vector.tensor_copy(d_w_picked[:], d_w[:].bitcast(U32).indirect(k1_t[:]))
        x1_w = new("x1_w", [P, S], U32, tag="x1_w_then_w2")
        nc.vector.tensor_copy(x1_w[:], x_w[:].bitcast(U32).indirect(offs_t[:]))
        d_w_dealt = new("d_w_dealt", [P, H], I32, tag="d_w_dealt_then_w1")
        deal(d_w_dealt[:], d_w_picked[:].bitcast(I32), 4)

        w_raw = [new("w1_raw", [P, N], I32, tag="d_w_then_w1"), new("w2_raw", [P, N], I32, tag="d_w_picked_then_w2")]
        nc.sync.dma_start(w_raw[0][:], as_words(w1_words))
        nc.sync.dma_start(w_raw[1][:], as_words(w2_words))

        for t in range(PACK):
            cols = slice(P * t, P * (t + 1))
            h_ps = psum.tile([P, S], F32, name="h_ps%d" % t, tag="bank%d" % t)
            nc.tensor.matmul_mx(
                h_ps[:], lhsT=d_w_dealt[:, cols].bitcast(FP8X4), lhsT_scale=plane1[:, cols],
                rhs=x1_w[:].bitcast(FP8X4), rhs_scale=plane1[:, H:], start=True, stop=True,
            )
            if t < 2:
                nc.scalar.activation(ping[t][:, :S], h_ps[:], COPY, scale=0.0625)
            else:
                nc.vector.tensor_scalar(ping[t][:, :S], h_ps[:], 0.0625, None, ALU.mult)
        x2_w = new("x2_w", [P, S], U32)
        nc.vector.tensor_copy(x2_w[:], x_w[:].bitcast(U32).indirect(two_t[:]))

        x2_sc = new("x2_sc", [P, S], U8)
        nc.vector.tensor_copy(x2_sc[:], x_sc[:].indirect(two_t[:]))
        staged2 = new("staged2", [P, 2 * N + S], U8, tag="plane1_then_staged2")
        deal(staged2[:, :N], w_sc[:, :N], 16)
        deal(staged2[:, N : 2 * N], w_sc[:, N:], 16)
        nc.vector.tensor_copy(staged2[:, 2 * N :].bitcast(I32), x2_sc[:].bitcast(I32))
        for q in range(QUADS):
            nc.sync.dma_start(
                plane2[32 * q : 32 * q + 4, :].bitcast(I32), staged2[32 * q : 32 * q + 32 : 8, :].bitcast(I32)
            )

        for t in range(PACK):
            nc.scalar.activation(pong[t][:, S:], ping[t][:].indirect(n1_t[:]), COPY)
            nc.vector.tensor_tensor(pong[t][:, :S], ping[t][:, :S], pong[t][:, S:], ALU.subtract)

        w_dealt = [new("w1_dealt", [P, N], I32, tag="d_w_dealt_then_w1"), new("w2_dealt", [P, N], I32, tag="x1_w_then_w2")]
        su_gain = new("su_gain", [P, PACK, S], F32)
        su = [new("su%d" % t, [P, S], F32) for t in range(PACK)]
        for t in range(PACK):
            nc.scalar.activation(ping[t][:, S:], pong[t][:].indirect(n2_t[:]), COPY)
            nc.vector.tensor_tensor(su[t][:], pong[t][:, :S], ping[t][:, S:], ALU.max)
            nc.vector.tensor_scalar(su_gain[:, t, :], su[t][:], gain[:, t : t + 1], None, ALU.mult)
            if t < 2:
                deal(w_dealt[t][:], w_raw[t][:], 4)

        h2_ps = [
            [psum.tile([P, HALF], F32, name="h2_ps%d_%d" % (u, t), tag="bank%d" % (PACK * (1 - u) + t)) for t in range(PACK)]
            for u in range(2)
        ]
        for u in range(2):
            places = slice(HALF * u, HALF * (u + 1))
            for t in range(PACK):
                cols = slice(P * t, P * (t + 1))
                nc.tensor.matmul_mx(
                    h2_ps[u][t][:], lhsT=w_dealt[1][:, cols].bitcast(FP8X4),
                    lhsT_scale=plane2[:, N + P * t : N + P * (t + 1)],
                    rhs=x2_w[:, places].bitcast(FP8X4),
                    rhs_scale=plane2[:, 2 * N + HALF * u : 2 * N + HALF * (u + 1)], start=True, stop=False,
                )

        z_w = new("z_w", [P, S], U32)
        z_sc = new("z_sc", [P, S], U8)
        for lo, hi in PIECES:
            picked = new("su_picked%d" % lo, [P, PACK, hi - lo], F32)
            for t in range(PACK):
                for a in range(lo, hi, 64):
                    nc.scalar.activation(
                        picked[:, t, a - lo : a - lo + 64], su_gain[:, t, :].indirect(n3_t[:, cols16(a, a + 64)]),
                        COPY, scale=0.5,
                    )
            z_bf = new("z_bf%d" % lo, [P, PACK * (hi - lo)], BF16)
            nc.vector.tensor_tensor(
                z_bf[:].rearrange("p (c i t) -> p c t i", i=4, t=PACK),
                su_gain[:, :, lo:hi].rearrange("p t (c i) -> p c t i", i=4),
                picked[:].rearrange("p t (c i) -> p c t i", i=4),
                ALU.add,
            )
            nc.vector.quantize_mx(z_w[:, lo:hi].bitcast(FP8X4), z_sc[:, lo:hi], z_bf[:])
            if hi % HALF == 0:
                u = hi // HALF - 1
                places = slice(HALF * u, HALF * (u + 1))
                for t in range(PACK):
                    cols = slice(P * t, P * (t + 1))
                    nc.tensor.matmul_mx(
                        h2_ps[u][t][:], lhsT=w_dealt[0][:, cols].bitcast(FP8X4), lhsT_scale=plane2[:, cols],
                        rhs=z_w[:, places].bitcast(FP8X4), rhs_scale=z_sc[:, places], start=False, stop=True,
                    )

        for t in range(PACK):
            nc.scalar.activation(ping[t][:, :HALF], h2_ps[0][t][:], COPY)
        for t in range(PACK):
            nc.vector.tensor_copy(ping[t][:, HALF:S], h2_ps[1][t][:])

        trimmed = new("trimmed", [P, PACK, S], F32)
        for t in range(PACK):
            nc.scalar.activation(pong[t][:, :S], ping[t][:].indirect(n5_t[:]), COPY)
            nc.scalar.activation(pong[t][:, S:], ping[t][:].indirect(n6_t[:]), COPY)
            larger = new("larger%d" % t, [P, S], F32)
            nc.vector.tensor_tensor(larger[:], pong[t][:, :S], pong[t][:, S:], ALU.max)
            nc.vector.tensor_tensor(trimmed[:, t, :], ping[t][:, :S], larger[:], ALU.subtract)

        y_w = new("y_w", [P, S], U32)
        y_sc = new("y_sc", [P, S], U8)
        out_rows = out_0.rearrange("(p t) j -> p t j", t=PACK)
        out_words = as_words(out_1)
        early = S - LAST
        picked = new("h2_picked", [P, PACK, early], F32)
        y = new("y", [P, PACK, early], F32)
        for t in range(PACK):
            nc.scalar.activation(picked[:, t, :], ping[t][:].indirect(n4_t[:, cols16(0, early)]), COPY)
            nc.vector.tensor_tensor(y[:, t, :], trimmed[:, t, :early], picked[:, t, :], ALU.add)
        nc.sync.dma_start(out_rows[:, :, :early], y[:])
        for lo, hi in ((0, HALF), (HALF, early)):
            y_bf = new("y_bf%d" % lo, [P, PACK * (hi - lo)], BF16)
            nc.vector.tensor_copy(
                y_bf[:].rearrange("p (c i t) -> p c t i", i=4, t=PACK),
                y[:, :, lo:hi].rearrange("p t (c i) -> p c t i", i=4),
            )
            nc.vector.quantize_mx(y_w[:, lo:hi].bitcast(FP8X4), y_sc[:, lo:hi], y_bf[:])
        nc.sync.dma_start(out_words[:, :early], y_w[:, :early].bitcast(I32))

        picked_last = new("h2_picked_last", [P, PACK, LAST], F32)
        for t in range(PACK):
            nc.scalar.activation(picked_last[:, t, :], ping[t][:].indirect(n4_t[:, cols16(early, S)]), COPY)
        y_bf_last = new("y_bf_last", [P, PACK * LAST], BF16)
        nc.vector.tensor_tensor(
            y_bf_last[:].rearrange("p (c i t) -> p c t i", i=4, t=PACK),
            trimmed[:, :, early:].rearrange("p t (c i) -> p c t i", i=4),
            picked_last[:].rearrange("p t (c i) -> p c t i", i=4),
            ALU.add,
        )
        y_last = new("y_last", [P, PACK, LAST], F32)
        nc.vector.tensor_tensor(y_last[:], trimmed[:, :, early:], picked_last[:], ALU.add)
        nc.vector.quantize_mx(y_w[:, early:].bitcast(FP8X4), y_sc[:, early:], y_bf_last[:])
        nc.scalar.dma_start(out_rows[:, :, early:], y_last[:])
        nc.sync.dma_start(out_words[:, early:], y_w[:, early:].bitcast(I32))
        for q in range(QUADS):
            queue = nc.scalar if q % 2 == 0 else nc.sync
            queue.dma_start(out_2[0, 4 * q : 4 * q + 4, :].bitcast(I32), y_sc[32 * q : 32 * q + 4, :].bitcast(I32))
